import numpy as np
import ml_dtypes


def mxq(x, axis, fmt="e4m3"):
    dtype, down = {"e4m3": (ml_dtypes.float8_e4m3fn, 7), "e5m2": (ml_dtypes.float8_e5m2, 14)}[fmt]
    v = np.moveaxis(np.asarray(x, np.float32).astype(ml_dtypes.bfloat16).astype(np.float64), axis, -1)
    blocks = v.reshape(v.shape[:-1] + (-1, 32))
    amax = np.abs(blocks).max(-1, keepdims=True)
    byte = np.maximum(np.where(amax > 0, np.frexp(amax)[1] - 1 + 127, 0) - down, 1)
    scale = np.exp2(byte - 127.0)
    codes = (blocks / scale).astype(np.float32).astype(dtype).astype(np.float64)
    return np.moveaxis((codes * scale).reshape(v.shape), -1, axis)


WIDE = False


def mx_kscale(k):
    if not WIDE:
        return np.ones(k)
    levels = np.array([10, -10, 5, -5, 0])
    if k % 512:
        return np.exp2(np.random.permutation(np.resize(levels, k // 32))).repeat(32)
    a = np.empty((k // 512, 16))
    for p in range(k // 512):
        a[p, :8] = np.random.permutation(np.resize(levels, 8))
        for g in range(8):
            far = levels[np.abs(levels - a[p, g]) >= 10]
            a[p, g + 8] = far[np.random.randint(len(far))]
    return np.exp2(a.ravel()).repeat(32)


def f64(x):
    return np.asarray(x).astype(np.float64)


def striped(idx):
    return np.tile(np.asarray(idx).reshape(-1, 16).T, (8, 1)).astype(np.uint16)


def unstriped(offs):
    return offs[:16].T.reshape(-1).astype(np.int64)


E2M1 = np.array([0.0, 0.5, 1.0, 1.5, 2.0, 3.0, 4.0, 6.0, -0.0, -0.5, -1.0, -1.5, -2.0, -3.0, -4.0, -6.0])


def pack_weight(w, fmt):
    k, n = w.shape
    w = f64(np.asarray(w, np.float32).astype(ml_dtypes.bfloat16)).reshape(k // 32, 32, n)
    amax = np.abs(w).max(1)
    if fmt == "e4m3":
        byte = np.frexp(amax)[1] - 1 + 127 - 7
    else:
        mant, ex = np.frexp(amax / 6.0)
        byte = np.where(mant > 0.5, ex, ex - 1) + 127
    byte = np.clip(np.where(amax > 0, byte, 1), 1, 254)
    scaled = (w * np.exp2(127.0 - byte)[:, None, :]).reshape(k, n).astype(np.float32)
    by_word = np.ascontiguousarray(scaled.reshape(k // 512, 128, 4, n).transpose(0, 1, 3, 2))
    if fmt == "e4m3":
        words = by_word.astype(ml_dtypes.float8_e4m3fn).view(np.uint8)
    else:
        c = by_word.astype(ml_dtypes.float4_e2m1fn).view(np.uint8) & 0xF
        words = (c[..., 0::2] | (c[..., 1::2] << 4)).reshape(k // 512, 128, 2 * n)
    return np.ascontiguousarray(words), np.ascontiguousarray(byte.astype(np.uint8).reshape(k // 512, 16, n))


def unpack_weight(words, scales, fmt):
    g, _, n = scales.shape
    words = np.ascontiguousarray(words).reshape(g, 128, n, -1)
    if fmt == "e4m3":
        vals = words.view(ml_dtypes.float8_e4m3fn).astype(np.float64)
    else:
        nib = np.empty((g, 128, n, 4), np.uint8)
        nib[..., 0::2] = words & 0xF
        nib[..., 1::2] = words >> 4
        vals = E2M1[nib]
    vals = vals * np.repeat(np.exp2(scales.astype(np.float64) - 127.0), 8, axis=1)[..., None]
    return vals.transpose(0, 1, 3, 2).reshape(g * 512, n)


def bf(x):
    return np.asarray(x, np.float32).astype(ml_dtypes.bfloat16)


def planes(Y):
    r, m = Y.shape
    b = f64(bf(Y)).reshape(r // 32, 32, m)
    amax = np.abs(b).max(1)
    byte = np.clip(np.where(amax > 0, np.frexp(amax)[1] - 1 + 127 - 7, 1), 1, 254)
    codes = (b * np.exp2(127.0 - byte)[:, None, :]).reshape(r, m).astype(np.float32).astype(ml_dtypes.float8_e4m3fn).view(np.uint8)
    words = codes.reshape(r // 512, 128, 4, m).transpose(0, 1, 3, 2)
    return np.ascontiguousarray(words), np.ascontiguousarray(byte.astype(np.uint8).reshape(r // 512, 16, m))


K, R, F, T, J, G = 512, 512, 512, 2048, 512, 64


def setup_inputs():
    n = np.random.standard_normal
    idx = np.random.permutation(T)[:J]
    fk = mx_kscale(K)
    ff = mx_kscale(F)
    tabp = pack_weight(n((K, T)) / fk[:, None], "e2m1")
    return {
        "tab_words": tabp[0],
        "tab_scales": tabp[1],
        "w1": (n((K, R)) * 1.5 / np.sqrt(K) * fk[:, None]).astype(np.float32),
        "w2": (n((K, R)) * 0.7 / np.sqrt(K) * fk[:, None]).astype(np.float32),
        "wo": (n((F, R)) * 1 / np.sqrt(F) * ff[:, None]).astype(np.float32),
        "dy": (n((F, G)) / ff[:, None]).astype(np.float32),
        "old": (0.5 * n((R, J))).astype(np.float32),
        "offs": striped(idx),
    }


def reference(tab_words, tab_scales, w1, w2, wo, dy, old, offs):
    idx = unstriped(offs)
    tabu = unpack_weight(tab_words, tab_scales, "e2m1")
    w1q = mxq(f64(w1), 0, "e4m3")
    tabidxg = tabu[:, idx]
    a = w1q.T @ tabidxg
    w2q = mxq(f64(w2), 0, "e4m3")
    b = w2q.T @ tabidxg
    p = np.exp(b)
    z = p.reshape(R, G, J // G).sum(axis=2)
    n1 = (p * a).reshape(R, G, J // G).sum(axis=2)
    u1 = np.tanh(n1 / z)
    woq = mxq(f64(wo), 0, "e4m3")
    dyq = mxq(f64(dy), 0, "e4m3")
    c0 = woq.T @ dyq
    dn1 = c0 * (1.0 - np.square(u1)) / z
    r1 = np.repeat(dn1, J // G, axis=1)
    da = r1 * p
    y = da * 4.0 + f64(old)
    words, scales = planes(y)
    return y, words, scales

from contextlib import ExitStack

import concourse.mybir as mybir
from concourse.masks import make_identity

K, R, F, T, J, G = 512, 512, 512, 2048, 512, 64
FLOPS = 2 * K * R * J * 2 + 2 * F * R * G

F32 = mybir.dt.float32
BF16 = mybir.dt.bfloat16
I32 = mybir.dt.int32
U32 = mybir.dt.uint32
U16 = mybir.dt.uint16
U8 = mybir.dt.uint8
FP8X4 = mybir.dt.float8_e4m3fn_x4
FP4X4 = mybir.dt.float4_e2m1fn_x4
ALU = mybir.AluOpType
ACT = mybir.ActivationFunctionType

P = 128
PACK = 4
HALVES = 2
JH = J // HALVES
GH = G // HALVES
GROUP = J // G


def tile_attend_cgatepool_a_pl_kernel(tc, tab_words, tab_scales, w1, w2, wo, dy, old, offs, out_0, out_1, out_2):
    nc = tc.nc
    with ExitStack() as ctx:
        keep = ctx.enter_context(tc.tile_pool(name="keep", bufs=1))
        psum = ctx.enter_context(tc.psum_pool(name="psum", bufs=1))

        def sb(name, shape, dtype):
            return keep.tile(shape, dtype, name=name, align_bytes=64)

        def bank(number, name, shape):
            return psum.tile(shape, F32, name=name, tag="bank%d" % number)

        offsets = sb("offsets", [P, J // 16], U16)
        nc.sync.dma_start(offsets[:], offs)
        words = sb("words", [P, T], U16)
        nc.sync.dma_start(out=words[:].bitcast(I32), in_=tab_words[0].bitcast(I32))
        scales = sb("scales", [P, T], U8)
        nc.gpsimd.memset(scales[:].bitcast(I32), 0)
        for q in range(4):
            nc.sync.dma_start(out=scales[q:P:32, :].bitcast(I32), in_=tab_scales[0, q:16:4, :].bitcast(I32))

        def load_weight(name, w):
            view = w.rearrange("(p j) c -> p j c", j=PACK)
            parts = []
            for h in range(2):
                raw = sb("%s_raw%d" % (name, h), [P, PACK, R // 2], F32)
                nc.sync.dma_start(out=raw[:], in_=view[:, :, h * (R // 2):(h + 1) * (R // 2)])
                parts.append(raw)
            return parts

        w2_raw = load_weight("w2", w2)
        w1_raw = load_weight("w1", w1)
        dy_raw = sb("dy_raw", [P, PACK, G], F32)
        nc.sync.dma_start(out=dy_raw[:], in_=dy.rearrange("(p j) g -> p j g", j=PACK))
        wo_raw = load_weight("wo", wo)
        old_sb = sb("old_sb", [P, PACK, J], F32)
        nc.sync.dma_start(out=old_sb[:], in_=old.rearrange("(p t) j -> p t j", t=PACK))

        ident = sb("ident", [P, P], F32)
        make_identity(nc, ident[:])

        tab_w = sb("tab_w", [P, J], U16)
        nc.vector.tensor_copy(tab_w[:], words[:].indirect(offsets[:]))
        tab_s = sb("tab_s", [P, J], U8)
        nc.vector.tensor_copy(tab_s[:], scales[:].indirect(offsets[:]))

        def deal(copy, grouped, raw, h):
            copy(out=grouped[:, :, 64 * h:64 * (h + 1), :].rearrange("p t m j -> p m j t"),
                 in_=raw[:].rearrange("p j (m t) -> p m j t", t=PACK))

        def quantise(name, grouped_flat, width):
            codes = sb(name + "_codes", [P, width], U32)
            plane = sb(name + "_plane", [P, width], U8)
            nc.vector.quantize_mx(out=codes[:].bitcast(FP8X4), scales=plane[:], in_=grouped_flat)
            return codes, plane

        def weight_mx(name, raw, copies):
            grouped = sb(name + "_bf", [P, PACK, P, PACK], BF16)
            for h in range(2):
                deal(copies[h], grouped, raw[h], h)
            return [quantise("%s%d" % (name, tp), grouped[:, 2 * tp:2 * tp + 2].rearrange("p t m j -> p (t m j)"), 2 * P)
                    for tp in range(2)]

        def branch(wq, h, tp, number, name):
            acc = bank(number, name, [P, 2, JH])
            cols = slice(h * JH, (h + 1) * JH)
            for tt in range(2):
                rows = slice(tt * P, (tt + 1) * P)
                nc.tensor.matmul_mx(out=acc[:, tt, :], lhsT=wq[tp][0][:, rows].bitcast(FP8X4), lhsT_scale=wq[tp][1][:, rows],
                                    rhs=tab_w[:, cols].bitcast(FP4X4), rhs_scale=tab_s[:, cols], start=True, stop=True)
            return acc[:].rearrange("p t (g q e) -> p q (t g) e", q=4, e=2)

        def group_sums(src, number, name):
            acc = bank(number, name, [P, P])
            for i in range(GROUP):
                nc.tensor.matmul(out=acc[:], lhsT=src[:, i // 2, :, i % 2], rhs=ident[:], is_transpose=True,
                                 start=(i == 0), stop=(i == GROUP - 1))
            return acc

        w2q = weight_mx("w2", w2_raw, (nc.scalar.copy, nc.vector.tensor_copy))
        p = [sb("p%d" % h, [P, 4, P, 2], F32) for h in range(HALVES)]
        pa = [sb("pa%d" % h, [P, 4, P, 2], F32) for h in range(HALVES)]
        b = [[branch(w2q, h, tp, 2 * h + tp, "b%d%d" % (h, tp)) for tp in range(2)] for h in range(HALVES)]
        w1q = weight_mx("w1", w1_raw, (nc.scalar.copy, nc.vector.tensor_copy))
        for h in range(HALVES):
            for tp in range(2):
                nc.scalar.activation(out=p[h][:, :, 64 * tp:64 * (tp + 1), :], in_=b[h][tp], func=ACT.Exp)
        dy_bf = sb("dy_bf", [P, G, PACK], BF16)
        nc.scalar.copy(out=dy_bf[:], in_=dy_raw[:].rearrange("p j g -> p g j"))
        wo_bf = sb("wo_bf", [P, PACK, P, PACK], BF16)
        for h in range(2):
            deal(nc.scalar.copy, wo_bf, wo_raw[h], h)

        def weigh(h, banks):
            for tp in range(2):
                a = branch(w1q, h, tp, banks[tp], "a%d%d" % (h, tp))
                part = slice(64 * tp, 64 * (tp + 1))
                nc.vector.tensor_tensor(out=pa[h][:, :, part, :], in0=a, in1=p[h][:, :, part, :], op=ALU.mult)

        def inverse(h, z):
            rz = sb("rz%d" % h, [P, P], F32)
            nc.vector.reciprocal(out=rz[:], in_=z[:])
            return rz

        def tanh_squared(h, n, rz):
            mean = sb("mean%d" % h, [P, P], F32)
            nc.vector.tensor_tensor(out=mean[:], in0=n[:], in1=rz[:], op=ALU.mult)
            u = sb("u%d" % h, [P, P], F32)
            nc.scalar.activation(out=u[:], in_=mean[:], func=ACT.Tanh)
            uu = sb("uu%d" % h, [P, P], F32)
            nc.scalar.activation(out=uu[:], in_=u[:], func=ACT.Square)
            return uu

        def turn_back(h, uu, rz):
            v = sb("v%d" % h, [P, P], F32)
            nc.vector.scalar_tensor_tensor(out=v[:], in0=uu[:], scalar=1.0, in1=rz[:], op0=ALU.subtract, op1=ALU.mult)
            vb = bank(4 + h, "vb%d" % h, [P, P])
            nc.tensor.transpose(vb[:], v[:], ident[:])
            return vb

        z0 = group_sums(p[0], 4, "z0")
        weigh(0, (6, 7))
        z1 = group_sums(p[1], 5, "z1")
        n0 = group_sums(pa[0], 2, "n0")
        rz0 = inverse(0, z0)
        weigh(1, (0, 1))
        n1 = group_sums(pa[1], 3, "n1")
        uu0 = tanh_squared(0, n0, rz0)
        dyq = quantise("dy", dy_bf[:].rearrange("p g j -> p (g j)"), G)
        woq = quantise("wo", wo_bf[:].rearrange("p t m j -> p (t m j)"), R)
        c0 = bank(6, "c0", [P, PACK, G])
        for t in range(PACK):
            rows = slice(t * P, (t + 1) * P)
            nc.tensor.matmul_mx(out=c0[:, t, :], lhsT=woq[0][:, rows].bitcast(FP8X4), lhsT_scale=woq[1][:, rows],
                                rhs=dyq[0][:].bitcast(FP8X4), rhs_scale=dyq[1][:], start=True, stop=True)
        c0n = sb("c0n", [P, HALVES, PACK, GH], F32)
        nc.scalar.activation(out=c0n[:], in_=c0[:].rearrange("p t (h g) -> p h t g", h=HALVES), func=ACT.Copy, scale=-4.0)
        vb0 = turn_back(0, uu0, rz0)
        rz1 = inverse(1, z1)
        uu1 = tanh_squared(1, n1, rz1)

        y_plane = sb("y_plane", [P, J], U8)
        out_view = out_0.rearrange("(p t) j -> p t j", t=PACK)
        words_view = out_1[0].rearrange("p c r -> p (c r)").bitcast(I32)

        def gradient(h, vb):
            d = sb("d%d" % h, [P, P], F32)
            nc.vector.tensor_tensor(out=d[:], in0=vb[:], in1=c0n[:, h].rearrange("p t g -> p (t g)"), op=ALU.mult)
            da = sb("da%d" % h, [P, PACK, JH], F32)
            nc.vector.tensor_tensor(out=da[:].rearrange("p t (g q e) -> p (t g) q e", q=4, e=2),
                                    in0=p[h][:].rearrange("p q n e -> p n q e"),
                                    in1=d[:].unsqueeze(2).unsqueeze(3).to_broadcast([P, P, 4, 2]), op=ALU.mult)
            return da

        def result(name, da, first, start, width, copy):
            cols = slice(start, start + width)
            y = sb("y" + name, [P, PACK, width], F32)
            nc.vector.tensor_tensor(out=y[:], in0=da[:, :, start - first:start - first + width], in1=old_sb[:, :, cols], op=ALU.add)
            nc.sync.dma_start(out=out_view[:, :, cols], in_=y[:])
            y_bf = sb("y_bf" + name, [P, width, PACK], BF16)
            copy(out=y_bf[:].rearrange("p (c i) t -> p c t i", i=4), in_=y[:].rearrange("p t (c i) -> p c t i", i=4))
            return y_bf

        y_codes = [sb("y_codes%d" % h, [P, JH], U32) for h in range(HALVES)]

        def planes(y_bf, start, width):
            h = start // JH
            nc.vector.quantize_mx(out=y_codes[h][:, start - h * JH:start - h * JH + width].bitcast(FP8X4),
                                  scales=y_plane[:, start:start + width], in_=y_bf[:].rearrange("p c t -> p (c t)"))

        da0 = gradient(0, vb0)
        vb1 = turn_back(1, uu1, rz1)
        yb0 = result("0", da0, 0, 0, JH, nc.scalar.copy)
        da1 = gradient(1, vb1)
        yb1 = result("1", da1, JH, JH, JH // 2, nc.scalar.copy)
        planes(yb0, 0, JH)
        nc.scalar.dma_start(out=words_view[:, 0:JH], in_=y_codes[0][:].bitcast(I32))
        yb2 = result("2", da1, JH, JH + JH // 2, JH // 2, nc.vector.tensor_copy)
        planes(yb1, JH, JH // 2)
        planes(yb2, JH + JH // 2, JH // 2)
        nc.sync.dma_start(out=words_view[:, JH:J], in_=y_codes[1][:].bitcast(I32))
        for q in range(4):
            queue = nc.scalar if q % 2 == 0 else nc.sync
            queue.dma_start(out=out_2[0, q:16:4, :].bitcast(I32), in_=y_plane[q:P:32, :].bitcast(I32))
